import numpy as np
import ml_dtypes


def mxq(x, axis, fmt="e4m3"):
    dtype, down = {"e4m3": (ml_dtypes.float8_e4m3fn, 7), "e5m2": (ml_dtypes.float8_e5m2, 14)}[fmt]
    v = np.moveaxis(np.asarray(x, np.float32).astype(ml_dtypes.bfloat16).astype(np.float64), axis, -1)
    blocks = v.reshape(v.shape[:-1] + (-1, 32))
    amax = np.abs(blocks).max(-1, keepdims=True)
    byte = np.maximum(np.where(amax > 0, np.frexp(amax)[1] - 1 + 127, 0) - down, 1)
    scale = np.exp2(byte - 127.0)
    codes = (blocks / scale).astype(np.float32).astype(dtype).astype(np.float64)
    return np.moveaxis((codes * scale).reshape(v.shape), -1, axis)


WIDE = False


def mx_kscale(k):
    if not WIDE:
        return np.ones(k)
    levels = np.array([10, -10, 5, -5, 0])
    if k % 512:
        return np.exp2(np.random.permutation(np.resize(levels, k // 32))).repeat(32)
    a = np.empty((k // 512, 16))
    for p in range(k // 512):
        a[p, :8] = np.random.permutation(np.resize(levels, 8))
        for g in range(8):
            far = levels[np.abs(levels - a[p, g]) >= 10]
            a[p, g + 8] = far[np.random.randint(len(far))]
    return np.exp2(a.ravel()).repeat(32)


BF16 = ml_dtypes.bfloat16


def bf(x):
    return np.asarray(x, np.float32).astype(BF16)


def f64(x):
    return np.asarray(x).astype(np.float64)


E2M1 = np.array([0.0, 0.5, 1.0, 1.5, 2.0, 3.0, 4.0, 6.0, -0.0, -0.5, -1.0, -1.5, -2.0, -3.0, -4.0, -6.0])


def pack_weight(w, fmt):
    k, n = w.shape
    w = f64(bf(w)).reshape(k // 32, 32, n)
    amax = np.abs(w).max(1)
    if fmt == "e4m3":
        byte = np.frexp(amax)[1] - 1 + 127 - 7
    else:
        mant, ex = np.frexp(amax / 6.0)
        byte = np.where(mant > 0.5, ex, ex - 1) + 127
    byte = np.clip(np.where(amax > 0, byte, 1), 1, 254)
    scaled = (w * np.exp2(127.0 - byte)[:, None, :]).reshape(k, n).astype(np.float32)
    by_word = np.ascontiguousarray(scaled.reshape(k // 512, 128, 4, n).transpose(0, 1, 3, 2))
    if fmt == "e4m3":
        words = by_word.astype(ml_dtypes.float8_e4m3fn).view(np.uint8)
    else:
        c = by_word.astype(ml_dtypes.float4_e2m1fn).view(np.uint8) & 0xF
        words = c[..., 0::2] | (c[..., 1::2] << 4)
    return np.ascontiguousarray(words), np.ascontiguousarray(byte.astype(np.uint8).reshape(k // 512, 16, n))


def unpack_weight(words, scales, fmt):
    g, p, n, _ = words.shape
    if fmt == "e4m3":
        vals = np.ascontiguousarray(words).view(ml_dtypes.float8_e4m3fn).astype(np.float64)
    else:
        nib = np.empty((g, p, n, 4), np.uint8)
        nib[..., 0::2] = words & 0xF
        nib[..., 1::2] = words >> 4
        vals = E2M1[nib]
    vals = vals * np.repeat(np.exp2(scales.astype(np.float64) - 127.0), 8, axis=1)[..., None]
    return vals.transpose(0, 1, 3, 2).reshape(g * 512, n)
def pack4(w):
    words, scales = pack_weight(w, "e2m1")
    return words.reshape(words.shape[0], 128, -1), scales


def unpack4(words, scales):
    return unpack_weight(words.reshape(words.shape[0], 128, -1, 2), scales, "e2m1")


def planes(Y):
    n, m = Y.shape
    b = f64(bf(Y)).reshape(n // 32, 32, m)
    amax = np.abs(b).max(1)
    byte = np.clip(np.where(amax > 0, np.frexp(amax)[1] - 1 + 127 - 7, 1), 1, 254)
    codes = (b * np.exp2(127.0 - byte)[:, None, :]).reshape(n, m).astype(np.float32).astype(ml_dtypes.float8_e4m3fn).view(np.uint8)
    words = codes.reshape(n // 512, 128, 4, m).transpose(0, 1, 3, 2)
    return np.ascontiguousarray(words), np.ascontiguousarray(byte.astype(np.uint8).reshape(n // 512, 16, m))


M, K, F, N = 768, 2048, 2048, 1024


def setup_inputs():
    rn = np.random.randn
    s = mx_kscale(K)
    t = mx_kscale(F)
    xt = rn(K, M) * s[:, None]
    w = rn(K, F) / np.sqrt(K) / s[:, None] * t[None, :]
    x_words, x_scales = pack_weight(xt, "e4m3")
    w_words, w_scales = pack4(w)
    return {
        "x_words": x_words,
        "x_scales": x_scales,
        "w_words": w_words,
        "w_scales": w_scales,
        "ref": bf(0.7 * rn(M, F) * t[None, :]),
        "pred": bf(rn(F, N) / np.sqrt(F) / t[:, None]),
        "u": bf(rn(M, N)),
        "rho": bf(0.5 * np.exp(0.3 * rn(N))),
        "step": bf(0.5 * np.exp(0.8 * rn(N))),
    }


def reference(x_words, x_scales, w_words, w_scales, ref, pred, u, rho, step):
    XT = unpack_weight(x_words, x_scales, "e4m3")
    W = unpack4(w_words, w_scales)
    E = (XT.T @ W) - f64(ref)
    G = mxq(E, 1, "e4m3") @ mxq(f64(pred), 0, "e4m3")
    y = (G + f64(rho) * f64(u)) * f64(step)
    words, scales = planes(y.T)
    return y, words, scales

@@ -1,0 +1,355 @@
+from contextlib import ExitStack
+
+import concourse.mybir as mybir
+from concourse.masks import make_identity
+
+M, K, F, N = 768, 2048, 2048, 1024
+FLOPS = 2 * M * K * F + 2 * M * F * N
+
+F32 = mybir.dt.float32
+BF16 = mybir.dt.bfloat16
+U32 = mybir.dt.uint32
+I32 = mybir.dt.int32
+U8 = mybir.dt.uint8
+FP8X4 = mybir.dt.float8_e4m3fn_x4
+FP4X4 = mybir.dt.float4_e2m1fn_x4
+ALU = mybir.AluOpType
+
+P = 128
+BANK = 512
+PASSES = 4
+ACC_BANKS = 4
+TURN_BANKS = 3
+
+LOADS = """
+rho:a step:a ident:g zx:v:06 zw:v:01 zw:v:12 zw:v:24 x:s:01 w:s:01 xs:s:06 ws:s:01 x:s:13 w:s:12 ws:s:12
+ref:s:0301 ref:s:0312 x:s:36 u:s:0601 ref:s:3601 ws:s:24 ref:s:3612 w:s:24 pred:s:30 pred:s:10 ref:s:0324
+pred:s:31 pred:s:20 pred:s:21 pred:s:00 ref:s:3624 pred:s:11 pred:s:01 u:s:0612
+"""
+
+PLAN = """
+bt:0 bt:1 bc:0 A:00 A:20 A:10 S:00 A:01 S:10 S:20 A:21 S:01 A:11 S:21 A:40 S:11 A:30 Rv:40 Rg:10 A:50 S:40
+A:41 Rg:30 S:50 S:30 T:00 Rg:20 T:10 S:41 V:00 T:20 Rv:00 A:31 V:10 V:20 Q:00 A:51 Q:10 S:31 Q:20 A:22 S:51
+Iv:301 Ia:300 T:30 T:50 T:40 V:30 A:12 Iv:100 V:50 P:30 V:40 A:13 Q:30 Ia:101 Q:50 S:22 A:02 S:12 S:13 Ia:311
+A:03 P:10 S:02 A:23 Ia:201 Q:40 Iv:200 A:32 Ia:310 S:03 S:23 T:11 P:20 T:01 V:11 T:21 P:31 A:43 V:01 Iv:210
+V:21 Q:11 A:42 Ia:000 Q:01 Q:21 S:32 A:52 Ia:001 S:42 S:43 A:53 Ia:211 S:52 P:00 A:33 Ia:110 S:53 P:21 S:33
+Ia:111 B:10 D:10 Ia:011 P:11 B:00 Rg:50 T:31 D:00 T:51 V:31 T:41 U:10 V:51 U:00 Ia:010 Q:31 B:20 Q:51 D:20
+C:10 B:30 P:01 V:41 D:30 C:00 B:50 Q:41 Rg:41 U:30 B:40 D:50 C:30 U:20 Rg:21 B:41 D:40 C:20 D:41 Rg:11 B:21
+U:50 D:21 Rg:01 B:11 U:40 X:020 X:240 D:11 Y:020 Rg:31 U:41 C:40 U:11 B:01 C:50 U:21 Rg:51 C:41 D:01 B:31
+Y:240 X:460 D:31 C:11 Z:240 Bh:511 Y:460 U:31 Bh:510 C:21 X:451 Z:020 U:01 C:31 Dh:510 Y:451 Dh:511 X:241 C:01
+Z:460 W:0 E:510 Y:241 E:511 X:021 Z:451 U:51 X:561 Y:021 Z:241 Y:561 Z:021 Z:561 W:1
+"""
+
+
+def tile_trajectory_cost_pullback_h2_kernel(
+    tc, x_words, x_scales, w_words, w_scales, ref, pred, u, rho, step, out_0, out_1, out_2
+):
+    nc = tc.nc
+    with ExitStack() as ctx:
+        keep = ctx.enter_context(tc.tile_pool(name="keep", bufs=1))
+        flow = ctx.enter_context(tc.tile_pool(name="flow", bufs=3))
+        psum = ctx.enter_context(tc.psum_pool(name="psum", bufs=1))
+        ctx.enter_context(tc.manual_schedule())
+
+        x_hbm = x_words.rearrange("g p m t -> p g (m t)").bitcast(I32)
+        w_hbm = w_words.bitcast(I32).rearrange("g p c -> p g c")
+        xs_hbm = x_scales.bitcast(I32).rearrange("g (q r) c -> r q g c", r=4)
+        ws_hbm = w_scales.bitcast(I32).rearrange("g (q r) c -> r q g c", r=4)
+        ref_hbm = ref.rearrange("(i p) f -> p i f", p=P)
+        u_hbm = u.rearrange("(i p) n -> p i n", p=P)
+        pred_hbm = pred.rearrange("(g p t) n -> g p t n", p=P, t=4)
+        codes_hbm = out_1.rearrange("h p m t -> h p (m t)").bitcast(I32)
+        scales_hbm = out_2.bitcast(I32).rearrange("h (q r) c -> h r q c", r=4)
+
+        queues = {"s": nc.sync, "a": nc.scalar, "g": nc.gpsimd}
+        movers = {"v": nc.vector, "g": nc.gpsimd}
+        x_sb, xs_sb, w_sb, ws_sb, ref_sb, u_sb, pred_sb, row_sb = {}, {}, {}, {}, {}, {}, {}, {}
+        planes = {}
+        live = {}
+        count = {"acc": 0, "turn": 0}
+
+        def bank(kind, shape):
+            banks = ACC_BANKS if kind == "acc" else TURN_BANKS
+            name = "%s%d" % (kind, count[kind] % banks)
+            count[kind] += 1
+            return psum.tile(shape, F32, name=name)
+
+        def zero_plane(kind, a, b, eng):
+            width = P if kind == "x" else BANK
+            plane = keep.tile([P, PASSES, (b - a) * width], U8, name="%ss%d" % (kind, a), align_bytes=64)
+            movers[eng].memset(plane[:].rearrange("p g c -> p (g c)").bitcast(I32), 0)
+            planes[kind, a] = plane
+            for i in range(a, b):
+                (xs_sb if kind == "x" else ws_sb)[i] = plane[:, :, (i - a) * width : (i - a + 1) * width]
+
+        def load_plane(kind, a, b, q):
+            words = (P if kind == "x" else BANK) // 4
+            hbm = xs_hbm if kind == "x" else ws_hbm
+            view = planes[kind, a][:].bitcast(I32)
+            for r in range(4):
+                queues[q].dma_start(out=view[r:P:32], in_=hbm[r, :, :, a * words : b * words])
+
+        def load_x(a, b, q):
+            t = keep.tile([P, PASSES, (b - a) * P], U32, name="x%d" % a, align_bytes=64)
+            queues[q].dma_start(out=t[:].bitcast(I32), in_=x_hbm[:, :, a * P : b * P])
+            for i in range(a, b):
+                x_sb[i] = t[:, :, (i - a) * P : (i - a + 1) * P]
+
+        def load_w(a, b, q):
+            t = keep.tile([P, PASSES, (b - a) * 2 * BANK], U8, name="w%d" % a, align_bytes=64)
+            queues[q].dma_start(out=t[:].bitcast(I32), in_=w_hbm[:, :, a * BANK // 2 : b * BANK // 2])
+            for j in range(a, b):
+                w_sb[j] = t[:, :, (j - a) * 2 * BANK : (j - a + 1) * 2 * BANK]
+
+        def load_rows(hbm, store, tag, a, b, c, d, q):
+            t = keep.tile([P, b - a, (d - c) * BANK], BF16, name="%s%d_%d" % (tag, a, c), align_bytes=64)
+            queues[q].dma_start(out=t[:], in_=hbm[:, a:b, c * BANK : d * BANK])
+            for i in range(a, b):
+                for j in range(c, d):
+                    store[i, j] = t[:, i - a, (j - c) * BANK : (j - c + 1) * BANK]
+
+        def load_pred(g, h, q):
+            t = keep.tile([P, 4, BANK], BF16, name="pred%d_%d" % (g, h), align_bytes=64)
+            queues[q].dma_start(out=t[:], in_=pred_hbm[g, :, :, h * BANK : (h + 1) * BANK])
+            pred_sb[g, h] = t
+
+        def load_vec(name, q):
+            t = keep.tile([P, 2, 4], BF16, name=name + "_rows", align_bytes=64)
+            queues[q].dma_start(out=t[:], in_=(rho if name == "rho" else step).rearrange("(h p t) -> p h t", p=P, t=4))
+            row_sb[name] = t
+
+        ident = keep.tile([P, P], F32, name="ident", align_bytes=64)
+        for item in LOADS.split():
+            part = item.split(":")
+            kind, q, n = part[0], part[1], [int(c) for c in (part[2] if len(part) > 2 else "")]
+            if kind == "zx" or kind == "zw":
+                zero_plane(kind[1], n[0], n[1], q)
+            elif kind == "xs" or kind == "ws":
+                load_plane(kind[0], n[0], n[1], q)
+            elif kind == "x":
+                load_x(n[0], n[1], q)
+            elif kind == "w":
+                load_w(n[0], n[1], q)
+            elif kind == "ref":
+                load_rows(ref_hbm, ref_sb, "ref", n[0], n[1], n[2], n[3], q)
+            elif kind == "u":
+                load_rows(u_hbm, u_sb, "u", n[0], n[1], n[2], n[3], q)
+            elif kind == "pred":
+                load_pred(n[0], n[1], q)
+            elif kind == "ident":
+                make_identity(nc, ident[:])
+            else:
+                load_vec(kind, q)
+
+        e_codes = keep.tile([P, M // P, PASSES * P], U32, name="e_codes", align_bytes=64)
+        e_scales = keep.tile([P, M // P, PASSES * P], U8, name="e_scales", align_bytes=64)
+        p_codes = keep.tile([P, PASSES, 2, BANK], U32, name="p_codes", align_bytes=64)
+        p_scales = keep.tile([P, PASSES, 2, BANK], U8, name="p_scales", align_bytes=64)
+        y_codes = keep.tile([P, 2, M], U32, name="y_codes", align_bytes=64)
+        y_scales = keep.tile([P, 2, M], U8, name="y_scales", align_bytes=64)
+        wide = {}
+        for name in ("rho",):
+            wide[name] = keep.tile([P, N], BF16, name=name + "_wide", align_bytes=64)
+
+        def paired(ap):
+            return ap.rearrange("m (p u e) -> m u p e", u=2, e=2)
+
+        def spread_turn(k):
+            name = ("rho", "step")[k]
+            words = row_sb[name][:].rearrange("p h t -> p (h t)").bitcast(F32)
+            b = bank("turn", [P, 4, P]) if k == 0 else psum.tile([P, 4, P], F32, name="step_bank")
+            for w in range(4):
+                nc.tensor.transpose(b[:, w, :], words[:, w : w + 1].to_broadcast([P, P]), ident[:])
+            live["spread", k] = b
+
+        def spread_copy(k):
+            name = ("rho", "step")[k]
+            out = wide[name][:].bitcast(F32).rearrange("m (h p u) -> m h p u", h=2, u=2)
+            nc.scalar.copy(out=out, in_=live["spread", k][:].rearrange("m (h u) p -> m h p u", u=2))
+
+        def step_pairs(h):
+            return live["spread", 1][:, 2 * h : 2 * h + 2, :].bitcast(BF16).rearrange("m u (p e) -> m u p e", e=2)
+
+        def first_product(i, j):
+            b = bank("acc", [P, BANK])
+            for g in range(PASSES):
+                nc.tensor.matmul_mx(
+                    out=b[:],
+                    lhsT=x_sb[i][:, g, :].bitcast(FP8X4),
+                    lhsT_scale=xs_sb[i][:, g, :],
+                    rhs=w_sb[j][:, g, :].bitcast(FP4X4),
+                    rhs_scale=ws_sb[j][:, g, :],
+                    start=(g == 0),
+                    stop=(g == PASSES - 1),
+                )
+            live["xw", i, j] = b
+
+        def subtract(i, j):
+            if j % 2 == 0:
+                live["e", i, j // 2] = flow.tile([P, 2, BANK], BF16, name="e_rows", bufs=6, align_bytes=64)
+            out = live["e", i, j // 2][:, j % 2, :].rearrange("m (u p e) -> m u p e", u=2, e=2)
+            nc.vector.tensor_tensor(out=out, in0=paired(live["xw", i, j][:]), in1=paired(ref_sb[i, j]), op=ALU.subtract)
+
+        def turn(rows):
+            b = bank("turn", [P, 2 * len(rows), P])
+            for k, row in enumerate(rows):
+                words = row.bitcast(F32)
+                for w in range(2):
+                    nc.tensor.transpose(b[:, 2 * k + w, :], words[:, w * P : (w + 1) * P], ident[:])
+            return b
+
+        def gather(b, name):
+            blocks = b.shape[1] // 2
+            t = flow.tile([P, blocks * BANK], BF16, name=name, align_bytes=64)
+            out = t[:].bitcast(F32).rearrange("p (k m u) -> p k m u", k=blocks, u=2)
+            nc.scalar.copy(out=out, in_=b[:].rearrange("p (k u) m -> p k m u", u=2))
+            return t
+
+        def turn_e(i, s):
+            live["et", i, s] = turn([live["e", i, s][:, 0, :], live["e", i, s][:, 1, :]])
+
+        def gather_e(i, s):
+            live["eg", i, s] = gather(live["et", i, s], "e_grouped")
+
+        def quantize_e(i, s):
+            cols = slice(2 * s * P, 2 * (s + 1) * P)
+            nc.vector.quantize_mx(out=e_codes[:, i, cols].bitcast(FP8X4), scales=e_scales[:, i, cols], in_=live["eg", i, s][:])
+
+        def interleave(g, h, part, on_vector):
+            if ("pg", g, h) not in live:
+                name = "p_grouped%d" % ((PASSES * h + g) % 4)
+                live["pg", g, h] = keep.tile([P, BANK, 4], BF16, name=name, align_bytes=64)
+            cols = slice(part * BANK // 2, (part + 1) * BANK // 2)
+            out = live["pg", g, h][:, cols, :].rearrange("p (c i) t -> p c t i", i=4)
+            src = pred_sb[g, h][:, :, cols].rearrange("p t (c i) -> p c t i", i=4)
+            if on_vector:
+                nc.vector.tensor_copy(out=out, in_=src)
+            else:
+                nc.scalar.copy(out=out, in_=src)
+
+        def quantize_pred(g, h):
+            nc.vector.quantize_mx(
+                out=p_codes[:, g, h, :].bitcast(FP8X4),
+                scales=p_scales[:, g, h, :],
+                in_=live["pg", g, h][:].rearrange("p n t -> p (n t)"),
+            )
+
+        def effort(i, h, eng, name, bufs):
+            t = flow.tile([P, BANK], F32, name=name, bufs=bufs)
+            eng.tensor_tensor(out=t[:], in0=u_sb[i, h], in1=wide["rho"][:, h * BANK : (h + 1) * BANK], op=ALU.mult)
+            live["ru", i, h] = t
+
+        def second_product(i, h):
+            b = bank("acc", [P, BANK])
+            for g in range(PASSES):
+                cols = slice(g * P, (g + 1) * P)
+                nc.tensor.matmul_mx(
+                    out=b[:],
+                    lhsT=e_codes[:, i, cols].bitcast(FP8X4),
+                    lhsT_scale=e_scales[:, i, cols],
+                    rhs=p_codes[:, g, h, :].bitcast(FP8X4),
+                    rhs_scale=p_scales[:, g, h, :],
+                    start=(g == 0),
+                    stop=(g == PASSES - 1),
+                )
+            live["g", i, h] = b
+
+        def add_effort(i, h):
+            t = flow.tile([P, BANK], F32, name="summed")
+            nc.vector.tensor_tensor(out=t[:], in0=live["g", i, h][:], in1=live["ru", i, h][:], op=ALU.add)
+            live["sum", i, h] = t
+
+        def scale(i, h):
+            t = flow.tile([P, BANK], F32, name="y", bufs=6)
+            order = "m (p u e) -> m p u e"
+            nc.vector.tensor_tensor(
+                out=t[:].rearrange(order, u=2, e=2),
+                in0=live["sum", i, h][:].rearrange(order, u=2, e=2),
+                in1=step_pairs(h).rearrange("m u p e -> m p u e"),
+                op=ALU.mult,
+            )
+            nc.sync.dma_start(out=out_0[i * P : (i + 1) * P, h * BANK : (h + 1) * BANK], in_=t[:])
+            live["y", i, h] = t
+
+        def round_y(i, h):
+            t = flow.tile([P, BANK], BF16, name="y_rows", bufs=4, align_bytes=64)
+            nc.scalar.copy(out=t[:].rearrange("m (u p e) -> m u p e", u=2, e=2), in_=paired(live["y", i, h][:]))
+            live["yr", i, h] = t
+
+        def second_half(i, h, half):
+            b = bank("acc", [P, BANK // 2])
+            n_cols = slice(half * BANK // 2, (half + 1) * BANK // 2)
+            for g in range(PASSES):
+                cols = slice(g * P, (g + 1) * P)
+                nc.tensor.matmul_mx(
+                    out=b[:],
+                    lhsT=e_codes[:, i, cols].bitcast(FP8X4),
+                    lhsT_scale=e_scales[:, i, cols],
+                    rhs=p_codes[:, g, h, n_cols].bitcast(FP8X4),
+                    rhs_scale=p_scales[:, g, h, n_cols],
+                    start=(g == 0),
+                    stop=(g == PASSES - 1),
+                )
+            live["g", i, h, half] = b
+
+        def add_half(i, h, half):
+            if half == 0:
+                live["sum", i, h] = flow.tile([P, BANK], F32, name="summed")
+            n_cols = slice(half * BANK // 2, (half + 1) * BANK // 2)
+            nc.vector.tensor_tensor(out=live["sum", i, h][:, n_cols], in0=live["g", i, h, half][:], in1=live["ru", i, h][:, n_cols], op=ALU.add)
+
+        def scale_round_half(i, h, half):
+            if half == 0:
+                live["yr", i, h] = flow.tile([P, BANK], BF16, name="y_last", bufs=1, align_bytes=64)
+            ps = slice(half * P // 2, (half + 1) * P // 2)
+            nc.vector.tensor_tensor(
+                out=live["yr", i, h][:].rearrange("m (u p e) -> m u p e", u=2, e=2)[:, :, ps, :],
+                in0=paired(live["sum", i, h][:])[:, :, ps, :],
+                in1=step_pairs(h)[:, :, ps, :],
+                op=ALU.mult,
+            )
+
+        def turn_y(a, b, h):
+            live["yt", a, h] = turn([live["yr", i, h][:] for i in range(a, b)])
+
+        def gather_y(a, b, h):
+            live["yg", a, h] = gather(live["yt", a, h], "y_grouped")
+
+        def quantize_y(a, b, h):
+            cols = slice(a * P, b * P)
+            nc.vector.quantize_mx(out=y_codes[:, h, cols].bitcast(FP8X4), scales=y_scales[:, h, cols], in_=live["yg", a, h][:])
+            nc.sync.dma_start(out=codes_hbm[h, :, cols], in_=y_codes[:, h, cols].bitcast(I32))
+
+        def store_scales(h):
+            view = y_scales[:, h, :].bitcast(I32)
+            for r in range(4):
+                nc.sync.dma_start(out=scales_hbm[h, r], in_=view[r:P:32])
+
+        steps = {
+            "bt": spread_turn,
+            "bc": spread_copy,
+            "A": first_product,
+            "S": subtract,
+            "T": turn_e,
+            "V": gather_e,
+            "Q": quantize_e,
+            "Ia": lambda g, h, part: interleave(g, h, part, False),
+            "Iv": lambda g, h, part: interleave(g, h, part, True),
+            "P": quantize_pred,
+            "Rv": lambda i, h: effort(i, h, nc.vector, "effort_v", 2),
+            "Rg": lambda i, h: effort(i, h, nc.gpsimd, "effort_g", 3),
+            "B": second_product,
+            "Bh": second_half,
+            "D": add_effort,
+            "Dh": add_half,
+            "E": scale_round_half,
+            "U": scale,
+            "C": round_y,
+            "X": turn_y,
+            "Y": gather_y,
+            "Z": quantize_y,
+            "W": store_scales,
+        }
+        for item in PLAN.split():
+            part = item.split(":")
+            steps[part[0]](*[int(c) for c in part[1]])

@@ -18,26 +18,28 @@ ALU = mybir.AluOpType
 P = 128
 BANK = 512
 PASSES = 4
+LAST_HALF = 1
 ACC_BANKS = 4
 TURN_BANKS = 3
 
 LOADS = """
-rho:a step:a ident:g zx:v:06 zw:v:01 zw:v:12 zw:v:24 x:s:01 w:s:01 xs:s:06 ws:s:01 x:s:13 w:s:12 ws:s:12
-ref:s:0301 ref:s:0312 x:s:36 u:s:0601 ref:s:3601 ws:s:24 ref:s:3612 w:s:24 pred:s:30 pred:s:10 ref:s:0324
-pred:s:31 pred:s:20 pred:s:21 pred:s:00 ref:s:3624 pred:s:11 pred:s:01 u:s:0612
+ident:g zx:v:03 zw:v:01 zw:v:12 zx:v:36 zw:v:24 x:s:13 rho:s step:s ws:s:01 wh:s:0 xs:s:03 wh:s:1 ws:s:12
+w:s:12 ref:s:0302 x:s:01 xs:s:36 x:s:36 u:s:3601 ref:s:3602 u:s:0301 ws:s:24 w:s:24 pred:s:30 ref:s:2324
+pred:s:20 ref:s:0124 pred:s:00 pred:s:10 ref:s:1224 pred:s:21 ref:s:5624 ref:s:3424 pred:s:01 pred:s:31
+u:s:0312 ref:s:4524 pred:s:11 u:s:3612
 """
 
 PLAN = """
-bt:0 bt:1 bc:0 A:00 A:20 A:10 S:00 A:01 S:10 S:20 A:21 S:01 A:11 S:21 A:40 S:11 A:30 Rv:40 Rg:10 A:50 S:40
-A:41 Rg:30 S:50 S:30 T:00 Rg:20 T:10 S:41 V:00 T:20 Rv:00 A:31 V:10 V:20 Q:00 A:51 Q:10 S:31 Q:20 A:22 S:51
-Iv:301 Ia:300 T:30 T:50 T:40 V:30 A:12 Iv:100 V:50 P:30 V:40 A:13 Q:30 Ia:101 Q:50 S:22 A:02 S:12 S:13 Ia:311
-A:03 P:10 S:02 A:23 Ia:201 Q:40 Iv:200 A:32 Ia:310 S:03 S:23 T:11 P:20 T:01 V:11 T:21 P:31 A:43 V:01 Iv:210
-V:21 Q:11 A:42 Ia:000 Q:01 Q:21 S:32 A:52 Ia:001 S:42 S:43 A:53 Ia:211 S:52 P:00 A:33 Ia:110 S:53 P:21 S:33
-Ia:111 B:10 D:10 Ia:011 P:11 B:00 Rg:50 T:31 D:00 T:51 V:31 T:41 U:10 V:51 U:00 Ia:010 Q:31 B:20 Q:51 D:20
-C:10 B:30 P:01 V:41 D:30 C:00 B:50 Q:41 Rg:41 U:30 B:40 D:50 C:30 U:20 Rg:21 B:41 D:40 C:20 D:41 Rg:11 B:21
-U:50 D:21 Rg:01 B:11 U:40 X:020 X:240 D:11 Y:020 Rg:31 U:41 C:40 U:11 B:01 C:50 U:21 Rg:51 C:41 D:01 B:31
-Y:240 X:460 D:31 C:11 Z:240 Bh:511 Y:460 U:31 Bh:510 C:21 X:451 Z:020 U:01 C:31 Dh:510 Y:451 Dh:511 X:241 C:01
-Z:460 W:0 E:510 Y:241 E:511 X:021 Z:451 U:51 X:561 Y:021 Z:241 Y:561 Z:021 Z:561 W:1
+bt:1 bt:0 bc:1 bc:0 A:20 A:10 A:21 S:20 A:11 S:10 S:21 S:11 A:00 S:00 A:01 T:20 S:01 T:10 V:20 V:10 Rg:50
+Rv:40 A:40 Rg:30 A:41 S:40 A:30 S:41 Rg:00 Q:20 A:51 Rg:20 A:50 S:30 S:50 A:31 S:51 T:00 Rg:10 T:40 S:31 V:00
+T:50 Q:10 V:40 Q:00 V:50 A:22 T:30 Iv:300 Ia:301 Q:40 S:22 A:23 V:30 Q:50 S:23 Ia:201 A:02 Q:30 P:30 A:03
+Ia:200 S:02 S:03 A:13 Ia:000 Iv:001 P:20 A:12 Ia:100 P:00 A:52 S:12 Ia:101 S:13 A:32 J:210 T:01 Ia:211 T:11
+S:52 T:21 S:32 V:01 P:10 V:21 A:33 V:11 Q:01 P:21 Ia:011 B:00 Q:21 S:33 Ia:010 Q:11 A:53 D:00 S:53 Rg:21
+Ia:310 A:42 U:00 S:42 A:43 C:00 P:01 Ia:311 S:43 B:10 T:51 Rv:11 T:31 V:51 D:10 T:41 V:31 P:31 V:41 Q:51 B:20
+Q:31 Ia:111 Q:41 D:20 B:30 Ia:110 U:10 Ug:20 D:30 B:40 C:10 D:40 P:11 B:50 X:020 D:50 Y:020 U:40 Rg:31 C:20
+B:21 U:30 C:40 U:50 Rg:01 C:30 B:31 D:21 C:50 D:31 B:11 Rg:41 U:21 X:240 D:11 Y:240 Rg:51 U:31 C:21 B:41 X:460
+U:11 D:41 C:31 Z:020 Y:460 B:01 U:41 Bh:510 Z:240 C:41 D:01 Bh:511 C:11 Z:460 W:0 X:451 U:01 X:241 Y:451
+Dh:510 C:01 Dh:511 F:510 Y:241 Z:451 X:021 E:510 E:511 Y:021 F:511 X:561 Z:241 Y:561 Z:021 Z:561 W:1
 """
 
 
@@ -99,7 +101,14 @@ def tile_trajectory_cost_pullback_h2_kernel(
             t = keep.tile([P, PASSES, (b - a) * 2 * BANK], U8, name="w%d" % a, align_bytes=64)
             queues[q].dma_start(out=t[:].bitcast(I32), in_=w_hbm[:, :, a * BANK // 2 : b * BANK // 2])
             for j in range(a, b):
-                w_sb[j] = t[:, :, (j - a) * 2 * BANK : (j - a + 1) * 2 * BANK]
+                for g in range(PASSES):
+                    w_sb[j, g] = t[:, g, (j - a) * 2 * BANK : (j - a + 1) * 2 * BANK]
+
+        def load_w_half(half, q):
+            t = keep.tile([P, 2, 2 * BANK], U8, name="w0_%d" % half, align_bytes=64)
+            queues[q].dma_start(out=t[:].bitcast(I32), in_=w_hbm[:, 2 * half : 2 * half + 2, 0 : BANK // 2])
+            for g in range(2):
+                w_sb[0, 2 * half + g] = t[:, g, :]
 
         def load_rows(hbm, store, tag, a, b, c, d, q):
             t = keep.tile([P, b - a, (d - c) * BANK], BF16, name="%s%d_%d" % (tag, a, c), align_bytes=64)
@@ -130,6 +139,13 @@ def tile_trajectory_cost_pullback_h2_kernel(
                 load_x(n[0], n[1], q)
             elif kind == "w":
                 load_w(n[0], n[1], q)
+            elif kind == "wh":
+                load_w_half(n[0], q)
+            elif kind == "predf":
+                t = keep.tile([P, 4, N], BF16, name="pred%d" % n[0], align_bytes=64)
+                queues[q].dma_start(out=t[:], in_=pred_hbm[n[0]])
+                for h in range(2):
+                    pred_sb[n[0], h] = t[:, :, h * BANK : (h + 1) * BANK]
             elif kind == "ref":
                 load_rows(ref_hbm, ref_sb, "ref", n[0], n[1], n[2], n[3], q)
             elif kind == "u":
@@ -148,7 +164,7 @@ def tile_trajectory_cost_pullback_h2_kernel(
         y_codes = keep.tile([P, 2, M], U32, name="y_codes", align_bytes=64)
         y_scales = keep.tile([P, 2, M], U8, name="y_scales", align_bytes=64)
         wide = {}
-        for name in ("rho",):
+        for name in ("rho", "step"):
             wide[name] = keep.tile([P, N], BF16, name=name + "_wide", align_bytes=64)
 
         def paired(ap):
@@ -177,7 +193,7 @@ def tile_trajectory_cost_pullback_h2_kernel(
                     out=b[:],
                     lhsT=x_sb[i][:, g, :].bitcast(FP8X4),
                     lhsT_scale=xs_sb[i][:, g, :],
-                    rhs=w_sb[j][:, g, :].bitcast(FP4X4),
+                    rhs=w_sb[j, g].bitcast(FP4X4),
                     rhs_scale=ws_sb[j][:, g, :],
                     start=(g == 0),
                     stop=(g == PASSES - 1),
@@ -186,7 +202,7 @@ def tile_trajectory_cost_pullback_h2_kernel(
 
         def subtract(i, j):
             if j % 2 == 0:
-                live["e", i, j // 2] = flow.tile([P, 2, BANK], BF16, name="e_rows", bufs=6, align_bytes=64)
+                live["e", i, j // 2] = flow.tile([P, 2, BANK], BF16, name="e_rows", bufs=5, align_bytes=64)
             out = live["e", i, j // 2][:, j % 2, :].rearrange("m (u p e) -> m u p e", u=2, e=2)
             nc.vector.tensor_tensor(out=out, in0=paired(live["xw", i, j][:]), in1=paired(ref_sb[i, j]), op=ALU.subtract)
 
@@ -217,12 +233,21 @@ def tile_trajectory_cost_pullback_h2_kernel(
 
         def interleave(g, h, part, on_vector):
             if ("pg", g, h) not in live:
-                name = "p_grouped%d" % ((PASSES * h + g) % 4)
+                name = "p_grouped%d" % (["00","10","20","30","01","11","21","31"].index("%d%d" % (g, h)) % 4)
                 live["pg", g, h] = keep.tile([P, BANK, 4], BF16, name=name, align_bytes=64)
             cols = slice(part * BANK // 2, (part + 1) * BANK // 2)
             out = live["pg", g, h][:, cols, :].rearrange("p (c i) t -> p c t i", i=4)
             src = pred_sb[g, h][:, :, cols].rearrange("p t (c i) -> p c t i", i=4)
-            if on_vector:
+            if on_vector == 2:
+                nc.gpsimd.tensor_scalar(
+                    out=live["pg", g, h][:, cols, :],
+                    in0=pred_sb[g, h][:, :, cols].rearrange("p t n -> p n t"),
+                    scalar1=1.0,
+                    scalar2=0.0,
+                    op0=ALU.mult,
+                    op1=ALU.add,
+                )
+            elif on_vector:
                 nc.vector.tensor_copy(out=out, in_=src)
             else:
                 nc.scalar.copy(out=out, in_=src)
@@ -255,12 +280,12 @@ def tile_trajectory_cost_pullback_h2_kernel(
             live["g", i, h] = b
 
         def add_effort(i, h):
-            t = flow.tile([P, BANK], F32, name="summed")
+            t = flow.tile([P, BANK], F32, name="summed", bufs=3)
             nc.vector.tensor_tensor(out=t[:], in0=live["g", i, h][:], in1=live["ru", i, h][:], op=ALU.add)
             live["sum", i, h] = t
 
         def scale(i, h):
-            t = flow.tile([P, BANK], F32, name="y", bufs=6)
+            t = flow.tile([P, BANK], F32, name="y", bufs=4)
             order = "m (p u e) -> m p u e"
             nc.vector.tensor_tensor(
                 out=t[:].rearrange(order, u=2, e=2),
@@ -271,9 +296,33 @@ def tile_trajectory_cost_pullback_h2_kernel(
             nc.sync.dma_start(out=out_0[i * P : (i + 1) * P, h * BANK : (h + 1) * BANK], in_=t[:])
             live["y", i, h] = t
 
-        def round_y(i, h):
+        def scale_on_gpsimd(i, h):
+            t = flow.tile([P, BANK], F32, name="y_g", bufs=2)
+            nc.gpsimd.tensor_tensor(out=t[:], in0=live["sum", i, h][:], in1=wide["step"][:, h * BANK : (h + 1) * BANK], op=ALU.mult)
+            nc.sync.dma_start(out=out_0[i * P : (i + 1) * P, h * BANK : (h + 1) * BANK], in_=t[:])
+            live["y", i, h] = t
+
+        def scale_half(i, h, half):
+            t = flow.tile([P, BANK // 2], F32, name="y_half", bufs=2)
+            ps = slice(half * P // 2, (half + 1) * P // 2)
+            n_cols = slice(half * BANK // 2, (half + 1) * BANK // 2)
+            order = "m (p u e) -> m p u e"
+            nc.vector.tensor_tensor(
+                out=t[:].rearrange(order, u=2, e=2),
+                in0=live["sum", i, h][:, n_cols].rearrange(order, u=2, e=2),
+                in1=step_pairs(h)[:, :, ps, :].rearrange("m u p e -> m p u e"),
+                op=ALU.mult,
+            )
+            n0 = h * BANK + half * BANK // 2
+            nc.sync.dma_start(out=out_0[i * P : (i + 1) * P, n0 : n0 + BANK // 2], in_=t[:])
+
+        def round_y(i, h, on_vector):
             t = flow.tile([P, BANK], BF16, name="y_rows", bufs=4, align_bytes=64)
-            nc.scalar.copy(out=t[:].rearrange("m (u p e) -> m u p e", u=2, e=2), in_=paired(live["y", i, h][:]))
+            out = t[:].rearrange("m (u p e) -> m u p e", u=2, e=2)
+            if on_vector:
+                nc.vector.tensor_copy(out=out, in_=paired(live["y", i, h][:]))
+            else:
+                nc.scalar.copy(out=out, in_=paired(live["y", i, h][:]))
             live["yr", i, h] = t
 
         def second_half(i, h, half):
@@ -294,7 +343,7 @@ def tile_trajectory_cost_pullback_h2_kernel(
 
         def add_half(i, h, half):
             if half == 0:
-                live["sum", i, h] = flow.tile([P, BANK], F32, name="summed")
+                live["sum", i, h] = flow.tile([P, BANK], F32, name="summed", bufs=3)
             n_cols = slice(half * BANK // 2, (half + 1) * BANK // 2)
             nc.vector.tensor_tensor(out=live["sum", i, h][:, n_cols], in0=live["g", i, h, half][:], in1=live["ru", i, h][:, n_cols], op=ALU.add)
 
@@ -335,16 +384,20 @@ def tile_trajectory_cost_pullback_h2_kernel(
             "Q": quantize_e,
             "Ia": lambda g, h, part: interleave(g, h, part, False),
             "Iv": lambda g, h, part: interleave(g, h, part, True),
+            "J": lambda g, h, part: interleave(g, h, part, 2),
             "P": quantize_pred,
             "Rv": lambda i, h: effort(i, h, nc.vector, "effort_v", 2),
-            "Rg": lambda i, h: effort(i, h, nc.gpsimd, "effort_g", 3),
+            "Rg": lambda i, h: effort(i, h, nc.gpsimd, "effort_g", 6),
             "B": second_product,
             "Bh": second_half,
             "D": add_effort,
             "Dh": add_half,
             "E": scale_round_half,
             "U": scale,
-            "C": round_y,
+            "Ug": scale_on_gpsimd,
+            "F": scale_half,
+            "C": lambda i, h: round_y(i, h, False),
+            "Cv": lambda i, h: round_y(i, h, True),
             "X": turn_y,
             "Y": gather_y,
             "Z": quantize_y,

from contextlib import ExitStack

import concourse.mybir as mybir
from concourse.masks import make_identity

M, K, F, N = 768, 2048, 2048, 1024
FLOPS = 2 * M * K * F + 2 * M * F * N

F32 = mybir.dt.float32
BF16 = mybir.dt.bfloat16
U32 = mybir.dt.uint32
I32 = mybir.dt.int32
U8 = mybir.dt.uint8
FP8X4 = mybir.dt.float8_e4m3fn_x4
FP4X4 = mybir.dt.float4_e2m1fn_x4
ALU = mybir.AluOpType

P = 128
BANK = 512
PASSES = 4
LAST_HALF = 1
ACC_BANKS = 4
TURN_BANKS = 3

LOADS = """
ident:g zx:v:03 zw:v:01 zw:v:12 zx:v:36 zw:v:24 x:s:13 rho:s step:s ws:s:01 wh:s:0 xs:s:03 wh:s:1 ws:s:12
w:s:12 ref:s:0302 x:s:01 xs:s:36 x:s:36 u:s:3601 ref:s:3602 u:s:0301 ws:s:24 w:s:24 pred:s:30 ref:s:2324
pred:s:20 ref:s:0124 pred:s:00 pred:s:10 ref:s:1224 pred:s:21 ref:s:5624 ref:s:3424 pred:s:01 pred:s:31
u:s:0312 ref:s:4524 pred:s:11 u:s:3612
"""

PLAN = """
bt:1 bt:0 bc:1 bc:0 A:20 A:10 A:21 S:20 A:11 S:10 S:21 S:11 A:00 S:00 A:01 T:20 S:01 T:10 V:20 V:10 Rg:50
Rv:40 A:40 Rg:30 A:41 S:40 A:30 S:41 Rg:00 Q:20 A:51 Rg:20 A:50 S:30 S:50 A:31 S:51 T:00 Rg:10 T:40 S:31 V:00
T:50 Q:10 V:40 Q:00 V:50 A:22 T:30 Iv:300 Ia:301 Q:40 S:22 A:23 V:30 Q:50 S:23 Ia:201 A:02 Q:30 P:30 A:03
Ia:200 S:02 S:03 A:13 Ia:000 Iv:001 P:20 A:12 Ia:100 P:00 A:52 S:12 Ia:101 S:13 A:32 J:210 T:01 Ia:211 T:11
S:52 T:21 S:32 V:01 P:10 V:21 A:33 V:11 Q:01 P:21 Ia:011 B:00 Q:21 S:33 Ia:010 Q:11 A:53 D:00 S:53 Rg:21
Ia:310 A:42 U:00 S:42 A:43 C:00 P:01 Ia:311 S:43 B:10 T:51 Rv:11 T:31 V:51 D:10 T:41 V:31 P:31 V:41 Q:51 B:20
Q:31 Ia:111 Q:41 D:20 B:30 Ia:110 U:10 Ug:20 D:30 B:40 C:10 D:40 P:11 B:50 X:020 D:50 Y:020 U:40 Rg:31 C:20
B:21 U:30 C:40 U:50 Rg:01 C:30 B:31 D:21 C:50 D:31 B:11 Rg:41 U:21 X:240 D:11 Y:240 Rg:51 U:31 C:21 B:41 X:460
U:11 D:41 C:31 Z:020 Y:460 B:01 U:41 Bh:510 Z:240 C:41 D:01 Bh:511 C:11 Z:460 W:0 X:451 U:01 X:241 Y:451
Dh:510 C:01 Dh:511 F:510 Y:241 Z:451 X:021 E:510 E:511 Y:021 F:511 X:561 Z:241 Y:561 Z:021 Z:561 W:1
"""


def tile_trajectory_cost_pullback_h2_kernel(
    tc, x_words, x_scales, w_words, w_scales, ref, pred, u, rho, step, out_0, out_1, out_2
):
    nc = tc.nc
    with ExitStack() as ctx:
        keep = ctx.enter_context(tc.tile_pool(name="keep", bufs=1))
        flow = ctx.enter_context(tc.tile_pool(name="flow", bufs=3))
        psum = ctx.enter_context(tc.psum_pool(name="psum", bufs=1))
        ctx.enter_context(tc.manual_schedule())

        x_hbm = x_words.rearrange("g p m t -> p g (m t)").bitcast(I32)
        w_hbm = w_words.bitcast(I32).rearrange("g p c -> p g c")
        xs_hbm = x_scales.bitcast(I32).rearrange("g (q r) c -> r q g c", r=4)
        ws_hbm = w_scales.bitcast(I32).rearrange("g (q r) c -> r q g c", r=4)
        ref_hbm = ref.rearrange("(i p) f -> p i f", p=P)
        u_hbm = u.rearrange("(i p) n -> p i n", p=P)
        pred_hbm = pred.rearrange("(g p t) n -> g p t n", p=P, t=4)
        codes_hbm = out_1.rearrange("h p m t -> h p (m t)").bitcast(I32)
        scales_hbm = out_2.bitcast(I32).rearrange("h (q r) c -> h r q c", r=4)

        queues = {"s": nc.sync, "a": nc.scalar, "g": nc.gpsimd}
        movers = {"v": nc.vector, "g": nc.gpsimd}
        x_sb, xs_sb, w_sb, ws_sb, ref_sb, u_sb, pred_sb, row_sb = {}, {}, {}, {}, {}, {}, {}, {}
        planes = {}
        live = {}
        count = {"acc": 0, "turn": 0}

        def bank(kind, shape):
            banks = ACC_BANKS if kind == "acc" else TURN_BANKS
            name = "%s%d" % (kind, count[kind] % banks)
            count[kind] += 1
            return psum.tile(shape, F32, name=name)

        def zero_plane(kind, a, b, eng):
            width = P if kind == "x" else BANK
            plane = keep.tile([P, PASSES, (b - a) * width], U8, name="%ss%d" % (kind, a), align_bytes=64)
            movers[eng].memset(plane[:].rearrange("p g c -> p (g c)").bitcast(I32), 0)
            planes[kind, a] = plane
            for i in range(a, b):
                (xs_sb if kind == "x" else ws_sb)[i] = plane[:, :, (i - a) * width : (i - a + 1) * width]

        def load_plane(kind, a, b, q):
            words = (P if kind == "x" else BANK) // 4
            hbm = xs_hbm if kind == "x" else ws_hbm
            view = planes[kind, a][:].bitcast(I32)
            for r in range(4):
                queues[q].dma_start(out=view[r:P:32], in_=hbm[r, :, :, a * words : b * words])

        def load_x(a, b, q):
            t = keep.tile([P, PASSES, (b - a) * P], U32, name="x%d" % a, align_bytes=64)
            queues[q].dma_start(out=t[:].bitcast(I32), in_=x_hbm[:, :, a * P : b * P])
            for i in range(a, b):
                x_sb[i] = t[:, :, (i - a) * P : (i - a + 1) * P]

        def load_w(a, b, q):
            t = keep.tile([P, PASSES, (b - a) * 2 * BANK], U8, name="w%d" % a, align_bytes=64)
            queues[q].dma_start(out=t[:].bitcast(I32), in_=w_hbm[:, :, a * BANK // 2 : b * BANK // 2])
            for j in range(a, b):
                for g in range(PASSES):
                    w_sb[j, g] = t[:, g, (j - a) * 2 * BANK : (j - a + 1) * 2 * BANK]

        def load_w_half(half, q):
            t = keep.tile([P, 2, 2 * BANK], U8, name="w0_%d" % half, align_bytes=64)
            queues[q].dma_start(out=t[:].bitcast(I32), in_=w_hbm[:, 2 * half : 2 * half + 2, 0 : BANK // 2])
            for g in range(2):
                w_sb[0, 2 * half + g] = t[:, g, :]

        def load_rows(hbm, store, tag, a, b, c, d, q):
            t = keep.tile([P, b - a, (d - c) * BANK], BF16, name="%s%d_%d" % (tag, a, c), align_bytes=64)
            queues[q].dma_start(out=t[:], in_=hbm[:, a:b, c * BANK : d * BANK])
            for i in range(a, b):
                for j in range(c, d):
                    store[i, j] = t[:, i - a, (j - c) * BANK : (j - c + 1) * BANK]

        def load_pred(g, h, q):
            t = keep.tile([P, 4, BANK], BF16, name="pred%d_%d" % (g, h), align_bytes=64)
            queues[q].dma_start(out=t[:], in_=pred_hbm[g, :, :, h * BANK : (h + 1) * BANK])
            pred_sb[g, h] = t

        def load_vec(name, q):
            t = keep.tile([P, 2, 4], BF16, name=name + "_rows", align_bytes=64)
            queues[q].dma_start(out=t[:], in_=(rho if name == "rho" else step).rearrange("(h p t) -> p h t", p=P, t=4))
            row_sb[name] = t

        ident = keep.tile([P, P], F32, name="ident", align_bytes=64)
        for item in LOADS.split():
            part = item.split(":")
            kind, q, n = part[0], part[1], [int(c) for c in (part[2] if len(part) > 2 else "")]
            if kind == "zx" or kind == "zw":
                zero_plane(kind[1], n[0], n[1], q)
            elif kind == "xs" or kind == "ws":
                load_plane(kind[0], n[0], n[1], q)
            elif kind == "x":
                load_x(n[0], n[1], q)
            elif kind == "w":
                load_w(n[0], n[1], q)
            elif kind == "wh":
                load_w_half(n[0], q)
            elif kind == "predf":
                t = keep.tile([P, 4, N], BF16, name="pred%d" % n[0], align_bytes=64)
                queues[q].dma_start(out=t[:], in_=pred_hbm[n[0]])
                for h in range(2):
                    pred_sb[n[0], h] = t[:, :, h * BANK : (h + 1) * BANK]
            elif kind == "ref":
                load_rows(ref_hbm, ref_sb, "ref", n[0], n[1], n[2], n[3], q)
            elif kind == "u":
                load_rows(u_hbm, u_sb, "u", n[0], n[1], n[2], n[3], q)
            elif kind == "pred":
                load_pred(n[0], n[1], q)
            elif kind == "ident":
                make_identity(nc, ident[:])
            else:
                load_vec(kind, q)

        e_codes = keep.tile([P, M // P, PASSES * P], U32, name="e_codes", align_bytes=64)
        e_scales = keep.tile([P, M // P, PASSES * P], U8, name="e_scales", align_bytes=64)
        p_codes = keep.tile([P, PASSES, 2, BANK], U32, name="p_codes", align_bytes=64)
        p_scales = keep.tile([P, PASSES, 2, BANK], U8, name="p_scales", align_bytes=64)
        y_codes = keep.tile([P, 2, M], U32, name="y_codes", align_bytes=64)
        y_scales = keep.tile([P, 2, M], U8, name="y_scales", align_bytes=64)
        wide = {}
        for name in ("rho", "step"):
            wide[name] = keep.tile([P, N], BF16, name=name + "_wide", align_bytes=64)

        def paired(ap):
            return ap.rearrange("m (p u e) -> m u p e", u=2, e=2)

        def spread_turn(k):
            name = ("rho", "step")[k]
            words = row_sb[name][:].rearrange("p h t -> p (h t)").bitcast(F32)
            b = bank("turn", [P, 4, P]) if k == 0 else psum.tile([P, 4, P], F32, name="step_bank")
            for w in range(4):
                nc.tensor.transpose(b[:, w, :], words[:, w : w + 1].to_broadcast([P, P]), ident[:])
            live["spread", k] = b

        def spread_copy(k):
            name = ("rho", "step")[k]
            out = wide[name][:].bitcast(F32).rearrange("m (h p u) -> m h p u", h=2, u=2)
            nc.scalar.copy(out=out, in_=live["spread", k][:].rearrange("m (h u) p -> m h p u", u=2))

        def step_pairs(h):
            return live["spread", 1][:, 2 * h : 2 * h + 2, :].bitcast(BF16).rearrange("m u (p e) -> m u p e", e=2)

        def first_product(i, j):
            b = bank("acc", [P, BANK])
            for g in range(PASSES):
                nc.tensor.matmul_mx(
                    out=b[:],
                    lhsT=x_sb[i][:, g, :].bitcast(FP8X4),
                    lhsT_scale=xs_sb[i][:, g, :],
                    rhs=w_sb[j, g].bitcast(FP4X4),
                    rhs_scale=ws_sb[j][:, g, :],
                    start=(g == 0),
                    stop=(g == PASSES - 1),
                )
            live["xw", i, j] = b

        def subtract(i, j):
            if j % 2 == 0:
                live["e", i, j // 2] = flow.tile([P, 2, BANK], BF16, name="e_rows", bufs=5, align_bytes=64)
            out = live["e", i, j // 2][:, j % 2, :].rearrange("m (u p e) -> m u p e", u=2, e=2)
            nc.vector.tensor_tensor(out=out, in0=paired(live["xw", i, j][:]), in1=paired(ref_sb[i, j]), op=ALU.subtract)

        def turn(rows):
            b = bank("turn", [P, 2 * len(rows), P])
            for k, row in enumerate(rows):
                words = row.bitcast(F32)
                for w in range(2):
                    nc.tensor.transpose(b[:, 2 * k + w, :], words[:, w * P : (w + 1) * P], ident[:])
            return b

        def gather(b, name):
            blocks = b.shape[1] // 2
            t = flow.tile([P, blocks * BANK], BF16, name=name, align_bytes=64)
            out = t[:].bitcast(F32).rearrange("p (k m u) -> p k m u", k=blocks, u=2)
            nc.scalar.copy(out=out, in_=b[:].rearrange("p (k u) m -> p k m u", u=2))
            return t

        def turn_e(i, s):
            live["et", i, s] = turn([live["e", i, s][:, 0, :], live["e", i, s][:, 1, :]])

        def gather_e(i, s):
            live["eg", i, s] = gather(live["et", i, s], "e_grouped")

        def quantize_e(i, s):
            cols = slice(2 * s * P, 2 * (s + 1) * P)
            nc.vector.quantize_mx(out=e_codes[:, i, cols].bitcast(FP8X4), scales=e_scales[:, i, cols], in_=live["eg", i, s][:])

        def interleave(g, h, part, on_vector):
            if ("pg", g, h) not in live:
                name = "p_grouped%d" % (["00","10","20","30","01","11","21","31"].index("%d%d" % (g, h)) % 4)
                live["pg", g, h] = keep.tile([P, BANK, 4], BF16, name=name, align_bytes=64)
            cols = slice(part * BANK // 2, (part + 1) * BANK // 2)
            out = live["pg", g, h][:, cols, :].rearrange("p (c i) t -> p c t i", i=4)
            src = pred_sb[g, h][:, :, cols].rearrange("p t (c i) -> p c t i", i=4)
            if on_vector == 2:
                nc.gpsimd.tensor_scalar(
                    out=live["pg", g, h][:, cols, :],
                    in0=pred_sb[g, h][:, :, cols].rearrange("p t n -> p n t"),
                    scalar1=1.0,
                    scalar2=0.0,
                    op0=ALU.mult,
                    op1=ALU.add,
                )
            elif on_vector:
                nc.vector.tensor_copy(out=out, in_=src)
            else:
                nc.scalar.copy(out=out, in_=src)

        def quantize_pred(g, h):
            nc.vector.quantize_mx(
                out=p_codes[:, g, h, :].bitcast(FP8X4),
                scales=p_scales[:, g, h, :],
                in_=live["pg", g, h][:].rearrange("p n t -> p (n t)"),
            )

        def effort(i, h, eng, name, bufs):
            t = flow.tile([P, BANK], F32, name=name, bufs=bufs)
            eng.tensor_tensor(out=t[:], in0=u_sb[i, h], in1=wide["rho"][:, h * BANK : (h + 1) * BANK], op=ALU.mult)
            live["ru", i, h] = t

        def second_product(i, h):
            b = bank("acc", [P, BANK])
            for g in range(PASSES):
                cols = slice(g * P, (g + 1) * P)
                nc.tensor.matmul_mx(
                    out=b[:],
                    lhsT=e_codes[:, i, cols].bitcast(FP8X4),
                    lhsT_scale=e_scales[:, i, cols],
                    rhs=p_codes[:, g, h, :].bitcast(FP8X4),
                    rhs_scale=p_scales[:, g, h, :],
                    start=(g == 0),
                    stop=(g == PASSES - 1),
                )
            live["g", i, h] = b

        def add_effort(i, h):
            t = flow.tile([P, BANK], F32, name="summed", bufs=3)
            nc.vector.tensor_tensor(out=t[:], in0=live["g", i, h][:], in1=live["ru", i, h][:], op=ALU.add)
            live["sum", i, h] = t

        def scale(i, h):
            t = flow.tile([P, BANK], F32, name="y", bufs=4)
            order = "m (p u e) -> m p u e"
            nc.vector.tensor_tensor(
                out=t[:].rearrange(order, u=2, e=2),
                in0=live["sum", i, h][:].rearrange(order, u=2, e=2),
                in1=step_pairs(h).rearrange("m u p e -> m p u e"),
                op=ALU.mult,
            )
            nc.sync.dma_start(out=out_0[i * P : (i + 1) * P, h * BANK : (h + 1) * BANK], in_=t[:])
            live["y", i, h] = t

        def scale_on_gpsimd(i, h):
            t = flow.tile([P, BANK], F32, name="y_g", bufs=2)
            nc.gpsimd.tensor_tensor(out=t[:], in0=live["sum", i, h][:], in1=wide["step"][:, h * BANK : (h + 1) * BANK], op=ALU.mult)
            nc.sync.dma_start(out=out_0[i * P : (i + 1) * P, h * BANK : (h + 1) * BANK], in_=t[:])
            live["y", i, h] = t

        def scale_half(i, h, half):
            t = flow.tile([P, BANK // 2], F32, name="y_half", bufs=2)
            ps = slice(half * P // 2, (half + 1) * P // 2)
            n_cols = slice(half * BANK // 2, (half + 1) * BANK // 2)
            order = "m (p u e) -> m p u e"
            nc.vector.tensor_tensor(
                out=t[:].rearrange(order, u=2, e=2),
                in0=live["sum", i, h][:, n_cols].rearrange(order, u=2, e=2),
                in1=step_pairs(h)[:, :, ps, :].rearrange("m u p e -> m p u e"),
                op=ALU.mult,
            )
            n0 = h * BANK + half * BANK // 2
            nc.sync.dma_start(out=out_0[i * P : (i + 1) * P, n0 : n0 + BANK // 2], in_=t[:])

        def round_y(i, h, on_vector):
            t = flow.tile([P, BANK], BF16, name="y_rows", bufs=4, align_bytes=64)
            out = t[:].rearrange("m (u p e) -> m u p e", u=2, e=2)
            if on_vector:
                nc.vector.tensor_copy(out=out, in_=paired(live["y", i, h][:]))
            else:
                nc.scalar.copy(out=out, in_=paired(live["y", i, h][:]))
            live["yr", i, h] = t

        def second_half(i, h, half):
            b = bank("acc", [P, BANK // 2])
            n_cols = slice(half * BANK // 2, (half + 1) * BANK // 2)
            for g in range(PASSES):
                cols = slice(g * P, (g + 1) * P)
                nc.tensor.matmul_mx(
                    out=b[:],
                    lhsT=e_codes[:, i, cols].bitcast(FP8X4),
                    lhsT_scale=e_scales[:, i, cols],
                    rhs=p_codes[:, g, h, n_cols].bitcast(FP8X4),
                    rhs_scale=p_scales[:, g, h, n_cols],
                    start=(g == 0),
                    stop=(g == PASSES - 1),
                )
            live["g", i, h, half] = b

        def add_half(i, h, half):
            if half == 0:
                live["sum", i, h] = flow.tile([P, BANK], F32, name="summed", bufs=3)
            n_cols = slice(half * BANK // 2, (half + 1) * BANK // 2)
            nc.vector.tensor_tensor(out=live["sum", i, h][:, n_cols], in0=live["g", i, h, half][:], in1=live["ru", i, h][:, n_cols], op=ALU.add)

        def scale_round_half(i, h, half):
            if half == 0:
                live["yr", i, h] = flow.tile([P, BANK], BF16, name="y_last", bufs=1, align_bytes=64)
            ps = slice(half * P // 2, (half + 1) * P // 2)
            nc.vector.tensor_tensor(
                out=live["yr", i, h][:].rearrange("m (u p e) -> m u p e", u=2, e=2)[:, :, ps, :],
                in0=paired(live["sum", i, h][:])[:, :, ps, :],
                in1=step_pairs(h)[:, :, ps, :],
                op=ALU.mult,
            )

        def turn_y(a, b, h):
            live["yt", a, h] = turn([live["yr", i, h][:] for i in range(a, b)])

        def gather_y(a, b, h):
            live["yg", a, h] = gather(live["yt", a, h], "y_grouped")

        def quantize_y(a, b, h):
            cols = slice(a * P, b * P)
            nc.vector.quantize_mx(out=y_codes[:, h, cols].bitcast(FP8X4), scales=y_scales[:, h, cols], in_=live["yg", a, h][:])
            nc.sync.dma_start(out=codes_hbm[h, :, cols], in_=y_codes[:, h, cols].bitcast(I32))

        def store_scales(h):
            view = y_scales[:, h, :].bitcast(I32)
            for r in range(4):
                nc.sync.dma_start(out=scales_hbm[h, r], in_=view[r:P:32])

        steps = {
            "bt": spread_turn,
            "bc": spread_copy,
            "A": first_product,
            "S": subtract,
            "T": turn_e,
            "V": gather_e,
            "Q": quantize_e,
            "Ia": lambda g, h, part: interleave(g, h, part, False),
            "Iv": lambda g, h, part: interleave(g, h, part, True),
            "J": lambda g, h, part: interleave(g, h, part, 2),
            "P": quantize_pred,
            "Rv": lambda i, h: effort(i, h, nc.vector, "effort_v", 2),
            "Rg": lambda i, h: effort(i, h, nc.gpsimd, "effort_g", 6),
            "B": second_product,
            "Bh": second_half,
            "D": add_effort,
            "Dh": add_half,
            "E": scale_round_half,
            "U": scale,
            "Ug": scale_on_gpsimd,
            "F": scale_half,
            "C": lambda i, h: round_y(i, h, False),
            "Cv": lambda i, h: round_y(i, h, True),
            "X": turn_y,
            "Y": gather_y,
            "Z": quantize_y,
            "W": store_scales,
        }
        for item in PLAN.split():
            part = item.split(":")
            steps[part[0]](*[int(c) for c in part[1]])
